import numpy as np
import ml_dtypes


def mxq(x, axis, fmt="e4m3"):
    dtype, down = {"e4m3": (ml_dtypes.float8_e4m3fn, 7), "e5m2": (ml_dtypes.float8_e5m2, 14)}[fmt]
    v = np.moveaxis(np.asarray(x, np.float32).astype(ml_dtypes.bfloat16).astype(np.float64), axis, -1)
    blocks = v.reshape(v.shape[:-1] + (-1, 32))
    amax = np.abs(blocks).max(-1, keepdims=True)
    byte = np.maximum(np.where(amax > 0, np.frexp(amax)[1] - 1 + 127, 0) - down, 1)
    scale = np.exp2(byte - 127.0)
    codes = (blocks / scale).astype(np.float32).astype(dtype).astype(np.float64)
    return np.moveaxis((codes * scale).reshape(v.shape), -1, axis)


WIDE = False


def mx_kscale(k):
    if not WIDE:
        return np.ones(k)
    levels = np.array([10, -10, 5, -5, 0])
    if k % 512:
        return np.exp2(np.random.permutation(np.resize(levels, k // 32))).repeat(32)
    a = np.empty((k // 512, 16))
    for p in range(k // 512):
        a[p, :8] = np.random.permutation(np.resize(levels, 8))
        for g in range(8):
            far = levels[np.abs(levels - a[p, g]) >= 10]
            a[p, g + 8] = far[np.random.randint(len(far))]
    return np.exp2(a.ravel()).repeat(32)


def f64(x):
    return np.asarray(x).astype(np.float64)


def striped(idx):
    return np.tile(np.asarray(idx).reshape(-1, 16).T, (8, 1)).astype(np.uint16)


def unstriped(offs):
    return offs[:16].T.reshape(-1).astype(np.int64)


E2M1 = np.array([0.0, 0.5, 1.0, 1.5, 2.0, 3.0, 4.0, 6.0, -0.0, -0.5, -1.0, -1.5, -2.0, -3.0, -4.0, -6.0])


def pack_weight(w, fmt):
    k, n = w.shape
    w = f64(np.asarray(w, np.float32).astype(ml_dtypes.bfloat16)).reshape(k // 32, 32, n)
    amax = np.abs(w).max(1)
    if fmt == "e4m3":
        byte = np.frexp(amax)[1] - 1 + 127 - 7
    else:
        mant, ex = np.frexp(amax / 6.0)
        byte = np.where(mant > 0.5, ex, ex - 1) + 127
    byte = np.clip(np.where(amax > 0, byte, 1), 1, 254)
    scaled = (w * np.exp2(127.0 - byte)[:, None, :]).reshape(k, n).astype(np.float32)
    by_word = np.ascontiguousarray(scaled.reshape(k // 512, 128, 4, n).transpose(0, 1, 3, 2))
    if fmt == "e4m3":
        words = by_word.astype(ml_dtypes.float8_e4m3fn).view(np.uint8)
    else:
        c = by_word.astype(ml_dtypes.float4_e2m1fn).view(np.uint8) & 0xF
        words = (c[..., 0::2] | (c[..., 1::2] << 4)).reshape(k // 512, 128, 2 * n)
    return np.ascontiguousarray(words), np.ascontiguousarray(byte.astype(np.uint8).reshape(k // 512, 16, n))


def unpack_weight(words, scales, fmt):
    g, _, n = scales.shape
    words = np.ascontiguousarray(words).reshape(g, 128, n, -1)
    if fmt == "e4m3":
        vals = words.view(ml_dtypes.float8_e4m3fn).astype(np.float64)
    else:
        nib = np.empty((g, 128, n, 4), np.uint8)
        nib[..., 0::2] = words & 0xF
        nib[..., 1::2] = words >> 4
        vals = E2M1[nib]
    vals = vals * np.repeat(np.exp2(scales.astype(np.float64) - 127.0), 8, axis=1)[..., None]
    return vals.transpose(0, 1, 3, 2).reshape(g * 512, n)


D, K, R, T, I, Q, G = 512, 512, 512, 2048, 512, 128, 32


def setup_inputs():
    n = np.random.standard_normal
    idx = np.random.permutation(T)[:I]
    fd = mx_kscale(D)
    fk = mx_kscale(K)
    fi = mx_kscale(I)
    keysp = pack_weight(n((D, T)) / fd[:, None], "e4m3")
    tabp = pack_weight(n((K, T)) / fk[:, None], "e4m3")
    return {
        "query": (n((D, Q)) * 0.7 / np.sqrt(D) * fd[:, None]).astype(np.float32),
        "keys_words": keysp[0],
        "keys_scales": keysp[1],
        "tab_words": tabp[0],
        "tab_scales": tabp[1],
        "w1": (n((K, R)) * 1 / np.sqrt(K) * fk[:, None]).astype(np.float32),
        "share": (np.random.uniform(0.4, 1.0, (R, 1))).astype(np.float32),
        "os": (np.random.uniform(4.0, 16.0, (1, I)) * fi).astype(np.float32),
        "vs": (np.random.uniform(0.5, 2.0, (1, I)) / fi).astype(np.float32),
        "offs": striped(idx),
    }


def reference(query, keys_words, keys_scales, tab_words, tab_scales, w1, share, os, vs, offs):
    idx = unstriped(offs)
    keysu = unpack_weight(keys_words, keys_scales, "e4m3")
    tabu = unpack_weight(tab_words, tab_scales, "e4m3")
    queryq = mxq(f64(query), 0, "e4m3")
    keysidxg = keysu[:, idx]
    a = queryq.T @ keysidxg
    p = np.exp(a - np.max(a, axis=1, keepdims=True))
    z = np.sum(p, axis=1, keepdims=True)
    w = p / z
    w1q = mxq(f64(w1), 0, "e4m3")
    tabidxg = tabu[:, idx]
    zh = w1q.T @ tabidxg
    mz = zh.reshape(R, G, I // G).mean(axis=2)
    mzr = np.repeat(mz, I // G, axis=1)
    hv = np.tanh(zh - mzr * f64(share))
    wo1 = w * f64(os)
    wt1 = wo1.T
    hw = hv * f64(vs)
    ht1 = hw.T
    wt1q = mxq(wt1, 0, "e4m3")
    ht1q = mxq(ht1, 0, "e4m3")
    o = wt1q.T @ ht1q
    return o

@@ -1,0 +1,225 @@
+from contextlib import ExitStack
+
+import concourse.mybir as mybir
+from concourse.masks import make_identity
+
+D, K, R, T, I, Q = 512, 512, 512, 2048, 512, 128
+PAGE = 16
+FLOPS = 2 * (Q * D * I + R * K * I + Q * I * R)
+
+F32 = mybir.dt.float32
+BF16 = mybir.dt.bfloat16
+I32 = mybir.dt.int32
+U32 = mybir.dt.uint32
+U16 = mybir.dt.uint16
+U8 = mybir.dt.uint8
+FP8X4 = mybir.dt.float8_e4m3fn_x4
+ACT = mybir.ActivationFunctionType
+ALU = mybir.AluOpType
+AX = mybir.AxisListType
+
+P = 128
+PACK = 4
+R_TILES = R // P
+W_HALVES = 2
+KEYS_ROW = 4
+
+
+def tile_attend_lrcentred_soft_kernel(tc, query, keys_words, keys_scales, tab_words, tab_scales, w1, share, slot_factor, value_scale, offs, out):
+    nc = tc.nc
+    with ExitStack() as ctx:
+        sb = ctx.enter_context(tc.tile_pool(name="sb", bufs=1))
+        ps = ctx.enter_context(tc.psum_pool(name="ps", bufs=1))
+
+        def tile(name, shape, dtype, tag=None):
+            return sb.tile(shape, dtype, name=name, tag=tag or name, align_bytes=64)
+
+        offsets = sb.tile([P, I // 16], U16, name="offsets")
+        keys_w = tile("keys_w", [P, T], U32)
+        keys_s = tile("keys_s", [P, T], U8)
+        tab_w = tile("tab_w", [P, T], U32)
+        tab_s = tile("tab_s", [P, T], U8)
+        q_raw = tile("q_raw", [P, PACK, Q], F32)
+        w_raw = [tile(f"w_raw{h}", [P, PACK, R // W_HALVES], F32) for h in range(W_HALVES)]
+        share_rows = tile("share_rows", [P, P], F32)
+        os_t = tile("os_t", [P, PACK], F32)
+        vs_t = tile("vs_t", [P, PACK], F32)
+        ident = tile("ident", [P, P], F32)
+
+        nc.vector.memset(tab_s[:].bitcast(I32), 0)
+        nc.vector.memset(keys_s[:].bitcast(I32), 0)
+
+        def load_words(dst, words):
+            nc.sync.dma_start(out=dst[:].bitcast(I32), in_=words[0].rearrange("p n t -> p (n t)").bitcast(I32))
+
+        def load_scales(dst, scales, first):
+            for r in range(4):
+                nc.sync.dma_start(out=dst[first + r : P : 32, :].bitcast(I32), in_=scales[0, r:16:4, :].bitcast(I32))
+
+        def load_w1(h):
+            cols = slice(h * (R // W_HALVES), (h + 1) * (R // W_HALVES))
+            nc.sync.dma_start(out=w_raw[h][:], in_=w1[:, cols].rearrange("(p j) c -> p j c", j=PACK))
+
+        nc.sync.dma_start(offsets[:], offs)
+        load_w1(0)
+        load_scales(tab_s, tab_scales, 0)
+        load_words(tab_w, tab_words)
+        nc.sync.dma_start(out=q_raw[:], in_=query.rearrange("(p j) q -> p j q", j=PACK))
+        load_scales(keys_s, keys_scales, KEYS_ROW)
+        load_w1(1)
+        load_words(keys_w, keys_words)
+        nc.sync.dma_start(out=vs_t[:], in_=value_scale.rearrange("o (p t) -> p (o t)", t=PACK))
+        nc.sync.dma_start(out=os_t[:], in_=slot_factor.rearrange("o (p t) -> p (o t)", t=PACK))
+        nc.gpsimd.memset(share_rows[:], 0.0)
+        make_identity(nc, ident[:])
+        nc.gpsimd.dma_start(out=share_rows[0:R_TILES, :], in_=share.rearrange("(j p) o -> j (p o)", p=P))
+
+        def gather(name, window, dtype):
+            picked = tile(name, [P, I], dtype)
+            nc.vector.tensor_copy(picked[:], window[:].indirect(offsets[:]))
+            return picked
+
+        def interleave(grouped, raw):
+            nc.scalar.activation(
+                out=grouped.rearrange("p (c i t) -> p c t i", i=4, t=PACK),
+                in_=raw.rearrange("p t (c i) -> p c t i", i=4),
+                func=ACT.Copy,
+            )
+
+        def quantise(name, grouped, tag=None):
+            width = grouped.shape[1] // PACK
+            codes = tile(name + "_codes", [P, width], U32, tag=tag)
+            scales = tile(name + "_scales", [P, width], U8)
+            nc.vector.quantize_mx(out=codes[:].bitcast(FP8X4), scales=scales[:], in_=grouped)
+            return codes, scales
+
+        def w1_bf(h):
+            grouped = tile(f"w_bf{h}", [P, 2 * P * PACK], BF16)
+            for e in range(2):
+                interleave(grouped[:, e * P * PACK : (e + 1) * P * PACK], w_raw[h][:, :, e * P : (e + 1) * P])
+            return grouped
+
+        def layer(j, w_op):
+            cols = slice((j % 2) * P, (j % 2 + 1) * P)
+            codes, scales = w_op
+            zh = ps.tile([P, I], F32, name=f"zh{j}", tag="zh", bufs=3)
+            nc.tensor.matmul_mx(out=zh[:], lhsT=codes[:, cols].bitcast(FP8X4), lhsT_scale=scales[:, cols],
+                                rhs=tab_g[:].bitcast(FP8X4), rhs_scale=tab_sg[:], start=True, stop=True)
+            return zh
+
+        def page_sums(zh, sums):
+            nc.vector.tensor_reduce(out=sums, in_=zh[:].rearrange("r (g u) -> r g u", u=PAGE), axis=AX.X, op=ALU.add)
+
+        def spread_shift(j, sums, shift):
+            nc.scalar.activation(out=shift.rearrange("r (g u) -> r g u", u=PAGE // PACK),
+                                 in_=sums.unsqueeze(2).to_broadcast([P, I // PAGE, PAGE // PACK]),
+                                 func=ACT.Copy, scale=pull[:, j : j + 1])
+
+        def deal(zh, zs):
+            nc.scalar.copy(out=zs.rearrange("r (t s) -> r t s", t=PACK), in_=zh[:].rearrange("r (s t) -> r t s", t=PACK))
+
+        def turn(j, shift, zs):
+            arg = ps.tile([P, PACK, P], F32, name=f"arg{j}", tag="arg", bufs=2)
+            for t in range(PACK):
+                nc.tensor.matmul(arg[:, t, :], lhsT=shift, rhs=ident[:],
+                                 is_transpose=True, start=(t == 0), stop=False)
+            for t in range(PACK):
+                nc.tensor.matmul(arg[:, t, :], lhsT=zs[:, t * P : (t + 1) * P], rhs=ident[:],
+                                 is_transpose=True, start=False, stop=(t == PACK - 1))
+            return arg
+
+        def squash(j, arg):
+            hv = tile(f"hv{j}", [P, P, PACK], F32)
+            nc.scalar.activation(out=hv[:], in_=arg[:].rearrange("s t r -> s r t"), func=ACT.Tanh)
+            return hv
+
+        def scale_values(j, hv):
+            nc.vector.tensor_tensor(out=ht_bf[:, j * I : (j + 1) * I].rearrange("s (r t) -> s r t", t=PACK), in0=hv[:],
+                                    in1=vs_t[:].unsqueeze(1).to_broadcast([P, P, PACK]), op=ALU.mult)
+
+        def read(j0, j1, h_op):
+            codes, scales = h_op
+            width = (j1 - j0) * P
+            acc = ps.tile([P, width], F32, name=f"acc{j0}", tag="acc", bufs=2)
+            nc.tensor.matmul_mx(out=acc[:], lhsT=wt_codes[:].bitcast(FP8X4), lhsT_scale=wt_scales[:],
+                                rhs=codes[:].bitcast(FP8X4), rhs_scale=scales[:], start=True, stop=True)
+            res = tile(f"res{j0}", [P, width], F32)
+            nc.scalar.copy(out=res[:], in_=acc[:])
+            nc.sync.dma_start(out=out[:, j0 * P : j1 * P], in_=res[:])
+
+        G = I // PAGE
+        share_cols = ps.tile([P, P], F32, name="share_cols", tag="acc", bufs=2)
+        nc.tensor.transpose(share_cols[:], share_rows[:], ident[:])
+        tab_sg = gather("tab_sg", tab_s, U8)
+        w_op01 = quantise("w01", w1_bf(0)[:], tag="tab_s")
+        tab_g = gather("tab_g", tab_w, U32)
+        zh0 = layer(0, w_op01)
+        zh1 = layer(1, w_op01)
+        q_bf = tile("q_bf", [P, Q * PACK], BF16)
+        interleave(q_bf[:], q_raw[:])
+        pull = tile("pull", [P, R_TILES], F32, tag="q_raw")
+        nc.scalar.activation(out=pull[:], in_=share_cols[:, :R_TILES], func=ACT.Copy, scale=-1.0 / PAGE)
+        q_codes, q_scales = quantise("q", q_bf[:])
+        keys_sg = gather("keys_sg", keys_s, U8)
+        w_bf23 = w1_bf(1)
+        sums0 = tile("sums0", [P, G], F32, tag="keys_s")
+        early = tile("early", [P, 2 * I + P], F32, tag="w_raw1")
+        zs0, zs1, shift0 = early[:, :I], early[:, I : 2 * I], early[:, 2 * I :]
+        page_sums(zh0, sums0[:])
+        w_op23 = quantise("w23", w_bf23[:])
+        zh2 = layer(2, w_op23)
+        spread_shift(0, sums0[:], shift0)
+        deal(zh0, zs0)
+        arg0 = turn(0, shift0, zs0)
+        sums1 = tile("sums1", [P, G], F32, tag="w_bf1")
+        page_sums(zh1, sums1[:])
+        deal(zh1, zs1)
+
+        keys_g = gather("keys_g", keys_w, U32)
+        late = tile("late", [P, 2 * I + P + 2 * G], F32, tag="keys_w")
+        ht_bf = late[:, : 2 * I].bitcast(BF16)
+        shift1 = late[:, 2 * I : 2 * I + P]
+        sums2, sums3 = late[:, 2 * I + P : 2 * I + P + G], late[:, 2 * I + P + G :]
+        scores = ps.tile([P, I], F32, name="scores", tag="soft")
+        nc.tensor.matmul_mx(out=scores[:], lhsT=q_codes[:].bitcast(FP8X4), lhsT_scale=q_scales[:],
+                            rhs=keys_g[:].bitcast(FP8X4), rhs_scale=keys_sg[KEYS_ROW:P, :], start=True, stop=True)
+        neg_max = tile("neg_max", [P, 1], F32)
+        nc.vector.tensor_reduce(out=neg_max[:], in_=scores[:], axis=AX.X, op=ALU.max, negate=True)
+        prob = tile("prob", [P, PACK, P], F32)
+        row_sum = tile("row_sum", [P, 1], F32)
+        nc.scalar.activation(out=prob[:], in_=scores[:].rearrange("q (s t) -> q t s", t=PACK), func=ACT.Exp,
+                             bias=neg_max[:], accum_out=row_sum[:])
+        inv_sum = tile("inv_sum", [P, 1], F32)
+        nc.vector.reciprocal(out=inv_sum[:], in_=row_sum[:])
+        weight = tile("weight", [P, PACK, P], F32)
+        nc.vector.tensor_scalar(out=weight[:], in0=prob[:], scalar1=inv_sum[:], scalar2=None, op0=ALU.mult)
+        weight_t = ps.tile([P, PACK, Q], F32, name="weight_t", tag="soft")
+        for t in range(PACK):
+            nc.tensor.transpose(weight_t[:, t, :], weight[:, t, :], ident[:])
+        wt_bf = tile("wt_bf", [P, Q, PACK], BF16)
+        nc.vector.tensor_tensor(out=wt_bf[:], in0=weight_t[:].rearrange("s t q -> s q t"),
+                                in1=os_t[:].unsqueeze(1).to_broadcast([P, Q, PACK]), op=ALU.mult)
+        wt_codes, wt_scales = quantise("wt", wt_bf[:].rearrange("s q t -> s (q t)"))
+
+        stage2 = tile("stage2", [P, I + P], F32)
+        stage3 = tile("stage3", [P, I + P], F32)
+        zh3 = layer(3, w_op23)
+        page_sums(zh2, sums2)
+        page_sums(zh3, sums3)
+        hv0 = squash(0, arg0)
+        spread_shift(1, sums1[:], shift1)
+        arg1 = turn(1, shift1, zs1)
+        spread_shift(2, sums2, stage2[:, I:])
+        deal(zh2, stage2[:, :I])
+        spread_shift(3, sums3, stage3[:, I:])
+        deal(zh3, stage3[:, :I])
+        arg2 = turn(2, stage2[:, I:], stage2[:, :I])
+        hv1 = squash(1, arg1)
+        arg3 = turn(3, stage3[:, I:], stage3[:, :I])
+        hv2 = squash(2, arg2)
+        hv3 = squash(3, arg3)
+        for j, hv in enumerate((hv0, hv1, hv2, hv3)):
+            scale_values(j, hv)
+        h_ops = [quantise(f"ht{j}", ht_bf[:, j * I : (j + 1) * I]) for j in range(R_TILES)]
+        for j in range(R_TILES):
+            read(j, j + 1, h_ops[j])

@@ -29,18 +29,24 @@ def tile_attend_lrcentred_soft_kernel(tc, query, keys_words, keys_scales, tab_wo
     nc = tc.nc
     with ExitStack() as ctx:
         sb = ctx.enter_context(tc.tile_pool(name="sb", bufs=1))
+        reused = ctx.enter_context(tc.tile_pool(name="reused", bufs=1))
         ps = ctx.enter_context(tc.psum_pool(name="ps", bufs=1))
 
-        def tile(name, shape, dtype, tag=None):
-            return sb.tile(shape, dtype, name=name, tag=tag or name, align_bytes=64)
+        def tile(name, shape, dtype, at=None):
+            if at is None:
+                return sb.tile(shape, dtype, name=name, align_bytes=64)
+            return reused.tile(shape, dtype, name=name, align_bytes=64, offset=at)
+
+        AT_TAB_S, AT_KEYS_S, AT_Q, AT_W, AT_KEYS_W = 0, 2048, 4096, 4096, 12288
+        G = I // PAGE
 
         offsets = sb.tile([P, I // 16], U16, name="offsets")
-        keys_w = tile("keys_w", [P, T], U32)
-        keys_s = tile("keys_s", [P, T], U8)
+        keys_w = tile("keys_w", [P, T], U32, AT_KEYS_W)
+        keys_s = tile("keys_s", [P, T], U8, AT_KEYS_S)
         tab_w = tile("tab_w", [P, T], U32)
-        tab_s = tile("tab_s", [P, T], U8)
+        tab_s = tile("tab_s", [P, T], U8, AT_TAB_S)
         q_raw = tile("q_raw", [P, PACK, Q], F32)
-        w_raw = [tile(f"w_raw{h}", [P, PACK, R // W_HALVES], F32) for h in range(W_HALVES)]
+        w_raw = [tile("w_raw0", [P, PACK, R // W_HALVES], F32), tile("w_raw1", [P, PACK, R // W_HALVES], F32, AT_W)]
         share_rows = tile("share_rows", [P, P], F32)
         os_t = tile("os_t", [P, PACK], F32)
         vs_t = tile("vs_t", [P, PACK], F32)
@@ -69,10 +75,10 @@ def tile_attend_lrcentred_soft_kernel(tc, query, keys_words, keys_scales, tab_wo
         load_w1(1)
         load_words(keys_w, keys_words)
         nc.sync.dma_start(out=vs_t[:], in_=value_scale.rearrange("o (p t) -> p (o t)", t=PACK))
-        nc.sync.dma_start(out=os_t[:], in_=slot_factor.rearrange("o (p t) -> p (o t)", t=PACK))
         nc.gpsimd.memset(share_rows[:], 0.0)
-        make_identity(nc, ident[:])
         nc.gpsimd.dma_start(out=share_rows[0:R_TILES, :], in_=share.rearrange("(j p) o -> j (p o)", p=P))
+        nc.gpsimd.dma_start(out=os_t[:], in_=slot_factor.rearrange("o (p t) -> p (o t)", t=PACK))
+        make_identity(nc, ident[:])
 
         def gather(name, window, dtype):
             picked = tile(name, [P, I], dtype)
@@ -86,9 +92,9 @@ def tile_attend_lrcentred_soft_kernel(tc, query, keys_words, keys_scales, tab_wo
                 func=ACT.Copy,
             )
 
-        def quantise(name, grouped, tag=None):
+        def quantise(name, grouped, at=None):
             width = grouped.shape[1] // PACK
-            codes = tile(name + "_codes", [P, width], U32, tag=tag)
+            codes = tile(name + "_codes", [P, width], U32, at)
             scales = tile(name + "_scales", [P, width], U8)
             nc.vector.quantize_mx(out=codes[:].bitcast(FP8X4), scales=scales[:], in_=grouped)
             return codes, scales
@@ -99,127 +105,131 @@ def tile_attend_lrcentred_soft_kernel(tc, query, keys_words, keys_scales, tab_wo
                 interleave(grouped[:, e * P * PACK : (e + 1) * P * PACK], w_raw[h][:, :, e * P : (e + 1) * P])
             return grouped
 
-        def layer(j, w_op):
-            cols = slice((j % 2) * P, (j % 2 + 1) * P)
-            codes, scales = w_op
+        def layer(j, codes, scales):
             zh = ps.tile([P, I], F32, name=f"zh{j}", tag="zh", bufs=3)
-            nc.tensor.matmul_mx(out=zh[:], lhsT=codes[:, cols].bitcast(FP8X4), lhsT_scale=scales[:, cols],
+            nc.tensor.matmul_mx(out=zh[:], lhsT=codes.bitcast(FP8X4), lhsT_scale=scales,
                                 rhs=tab_g[:].bitcast(FP8X4), rhs_scale=tab_sg[:], start=True, stop=True)
             return zh
 
-        def page_sums(zh, sums):
-            nc.vector.tensor_reduce(out=sums, in_=zh[:].rearrange("r (g u) -> r g u", u=PAGE), axis=AX.X, op=ALU.add)
+        def page_sums(j, zh, at=None):
+            sums = tile(f"sums{j}", [P, G], F32, at)
+            nc.vector.tensor_reduce(out=sums[:], in_=zh[:].rearrange("r (g u) -> r g u", u=PAGE), axis=AX.X, op=ALU.add)
+            return sums[:].unsqueeze(2).to_broadcast([P, G, PAGE // PACK])
 
-        def spread_shift(j, sums, shift):
-            nc.scalar.activation(out=shift.rearrange("r (g u) -> r g u", u=PAGE // PACK),
-                                 in_=sums.unsqueeze(2).to_broadcast([P, I // PAGE, PAGE // PACK]),
-                                 func=ACT.Copy, scale=pull[:, j : j + 1])
+        def spread_shift(j, sums, at=None):
+            shift = tile(f"shift{j}", [P, G, PAGE // PACK], F32, at)
+            nc.scalar.activation(out=shift[:], in_=sums, func=ACT.Copy, scale=pull[:, j : j + 1])
+            return [shift[:].rearrange("r g c -> r (g c)")] * PACK
 
-        def deal(zh, zs):
-            nc.scalar.copy(out=zs.rearrange("r (t s) -> r t s", t=PACK), in_=zh[:].rearrange("r (s t) -> r t s", t=PACK))
+        def deal(j, zh, at=None):
+            zs = tile(f"zs{j}", [P, PACK, P], F32, at)
+            nc.scalar.copy(out=zs[:], in_=zh[:].rearrange("r (s t) -> r t s", t=PACK))
+            return [zs[:, t, :] for t in range(PACK)]
 
-        def turn(j, shift, zs):
+        def turn_and_add(j, first, second):
             arg = ps.tile([P, PACK, P], F32, name=f"arg{j}", tag="arg", bufs=2)
             for t in range(PACK):
-                nc.tensor.matmul(arg[:, t, :], lhsT=shift, rhs=ident[:],
-                                 is_transpose=True, start=(t == 0), stop=False)
+                nc.tensor.matmul(arg[:, t, :], lhsT=first[t], rhs=ident[:], is_transpose=True, start=(t == 0), stop=False)
             for t in range(PACK):
-                nc.tensor.matmul(arg[:, t, :], lhsT=zs[:, t * P : (t + 1) * P], rhs=ident[:],
-                                 is_transpose=True, start=False, stop=(t == PACK - 1))
+                nc.tensor.matmul(arg[:, t, :], lhsT=second[t], rhs=ident[:], is_transpose=True, start=False, stop=(t == PACK - 1))
             return arg
 
-        def squash(j, arg):
-            hv = tile(f"hv{j}", [P, P, PACK], F32)
+        def shift_and_turn(j, sums, zh):
+            centred = tile(f"centred{j}", [P, PACK, G, PAGE // PACK], F32)
+            by_place = zh[:].rearrange("r (g c t) -> r t g c", c=PAGE // PACK, t=PACK)
+            arg = ps.tile([P, PACK, P], F32, name=f"arg{j}", tag="arg", bufs=2)
+            for t in range(PACK):
+                nc.vector.scalar_tensor_tensor(out=centred[:, t], in0=sums, scalar=pull[:, j : j + 1], in1=by_place[:, t],
+                                               op0=ALU.mult, op1=ALU.add)
+                nc.tensor.transpose(arg[:, t, :], centred[:, t].rearrange("r g c -> r (g c)"), ident[:])
+            return arg
+
+        def squash(j, arg, at=None):
+            hv = tile(f"hv{j}", [P, P, PACK], F32, at)
             nc.scalar.activation(out=hv[:], in_=arg[:].rearrange("s t r -> s r t"), func=ACT.Tanh)
             return hv
 
-        def scale_values(j, hv):
-            nc.vector.tensor_tensor(out=ht_bf[:, j * I : (j + 1) * I].rearrange("s (r t) -> s r t", t=PACK), in0=hv[:],
+        def scale_values(hv, ht_bf):
+            nc.vector.tensor_tensor(out=ht_bf.rearrange("s (r t) -> s r t", t=PACK), in0=hv[:],
                                     in1=vs_t[:].unsqueeze(1).to_broadcast([P, P, PACK]), op=ALU.mult)
 
-        def read(j0, j1, h_op):
+        def read(j0, h_op, bank, bufs, copy):
             codes, scales = h_op
-            width = (j1 - j0) * P
-            acc = ps.tile([P, width], F32, name=f"acc{j0}", tag="acc", bufs=2)
+            width = codes.shape[1]
+            acc = ps.tile([P, width], F32, name=f"acc{j0}", tag=bank, bufs=bufs)
             nc.tensor.matmul_mx(out=acc[:], lhsT=wt_codes[:].bitcast(FP8X4), lhsT_scale=wt_scales[:],
                                 rhs=codes[:].bitcast(FP8X4), rhs_scale=scales[:], start=True, stop=True)
             res = tile(f"res{j0}", [P, width], F32)
-            nc.scalar.copy(out=res[:], in_=acc[:])
-            nc.sync.dma_start(out=out[:, j0 * P : j1 * P], in_=res[:])
+            copy(out=res[:], in_=acc[:])
+            nc.sync.dma_start(out=out[:, j0 * P : j0 * P + width], in_=res[:])
 
-        G = I // PAGE
+        os_spread = ps.tile([P, PACK, P], F32, name="os_spread", tag="acc", bufs=2)
+        for t in range(PACK):
+            nc.tensor.transpose(os_spread[:, t, :], os_t[:, t : t + 1].to_broadcast([P, P]), ident[:])
         share_cols = ps.tile([P, P], F32, name="share_cols", tag="acc", bufs=2)
         nc.tensor.transpose(share_cols[:], share_rows[:], ident[:])
         tab_sg = gather("tab_sg", tab_s, U8)
-        w_op01 = quantise("w01", w1_bf(0)[:], tag="tab_s")
+        w01_codes, w01_scales = quantise("w01", w1_bf(0)[:], AT_TAB_S)
         tab_g = gather("tab_g", tab_w, U32)
-        zh0 = layer(0, w_op01)
-        zh1 = layer(1, w_op01)
+        zh0 = layer(0, w01_codes[:, :P], w01_scales[:, :P])
+        zh1 = layer(1, w01_codes[:, P:], w01_scales[:, P:])
         q_bf = tile("q_bf", [P, Q * PACK], BF16)
         interleave(q_bf[:], q_raw[:])
-        pull = tile("pull", [P, R_TILES], F32, tag="q_raw")
-        nc.scalar.activation(out=pull[:], in_=share_cols[:, :R_TILES], func=ACT.Copy, scale=-1.0 / PAGE)
-        q_codes, q_scales = quantise("q", q_bf[:])
         keys_sg = gather("keys_sg", keys_s, U8)
         w_bf23 = w1_bf(1)
-        sums0 = tile("sums0", [P, G], F32, tag="keys_s")
-        early = tile("early", [P, 2 * I + P], F32, tag="w_raw1")
-        zs0, zs1, shift0 = early[:, :I], early[:, I : 2 * I], early[:, 2 * I :]
-        page_sums(zh0, sums0[:])
-        w_op23 = quantise("w23", w_bf23[:])
-        zh2 = layer(2, w_op23)
-        spread_shift(0, sums0[:], shift0)
-        deal(zh0, zs0)
-        arg0 = turn(0, shift0, zs0)
-        sums1 = tile("sums1", [P, G], F32, tag="w_bf1")
-        page_sums(zh1, sums1[:])
-        deal(zh1, zs1)
+        pull = tile("pull", [P, R_TILES], F32, AT_W + 3200)
+        nc.scalar.activation(out=pull[:], in_=share_cols[:, :R_TILES], func=ACT.Copy, scale=-1.0 / PAGE)
+        sums0 = page_sums(0, zh0, AT_KEYS_S)
+        w2_codes, w2_scales = quantise("w2", w_bf23[:, : P * PACK])
+        zh2 = layer(2, w2_codes[:], w2_scales[:])
+        q_codes, q_scales = quantise("q", q_bf[:], AT_W + 2688)
+        zs0 = deal(0, zh0, AT_W)
+        arg0 = turn_and_add(0, zs0, spread_shift(0, sums0, AT_W + 2048))
+        sums1 = page_sums(1, zh1, AT_W + 2560)
+        zs1 = deal(1, zh1)
+        os_rows = tile("os_rows", [P, 2, P, 2], F32, AT_W + 3264)
+        nc.scalar.copy(out=os_rows[:], in_=os_spread[:].rearrange("q (u e) s -> q u s e", e=2))
 
         keys_g = gather("keys_g", keys_w, U32)
-        late = tile("late", [P, 2 * I + P + 2 * G], F32, tag="keys_w")
-        ht_bf = late[:, : 2 * I].bitcast(BF16)
-        shift1 = late[:, 2 * I : 2 * I + P]
-        sums2, sums3 = late[:, 2 * I + P : 2 * I + P + G], late[:, 2 * I + P + G :]
         scores = ps.tile([P, I], F32, name="scores", tag="soft")
         nc.tensor.matmul_mx(out=scores[:], lhsT=q_codes[:].bitcast(FP8X4), lhsT_scale=q_scales[:],
                             rhs=keys_g[:].bitcast(FP8X4), rhs_scale=keys_sg[KEYS_ROW:P, :], start=True, stop=True)
+        w3_codes, w3_scales = quantise("w3", w_bf23[:, P * PACK :], AT_KEYS_W)
+        zh3 = layer(3, w3_codes[:], w3_scales[:])
+        arg1 = turn_and_add(1, spread_shift(1, sums1, AT_KEYS_W + 512), zs1)
+        sums2 = page_sums(2, zh2, AT_KEYS_W + 1024)
+
         neg_max = tile("neg_max", [P, 1], F32)
         nc.vector.tensor_reduce(out=neg_max[:], in_=scores[:], axis=AX.X, op=ALU.max, negate=True)
-        prob = tile("prob", [P, PACK, P], F32)
+        prob = tile("prob", [P, 2, P, 2], F32)
         row_sum = tile("row_sum", [P, 1], F32)
-        nc.scalar.activation(out=prob[:], in_=scores[:].rearrange("q (s t) -> q t s", t=PACK), func=ACT.Exp,
+        nc.scalar.activation(out=prob[:], in_=scores[:].rearrange("q (s u e) -> q u s e", u=2, e=2), func=ACT.Exp,
                              bias=neg_max[:], accum_out=row_sum[:])
         inv_sum = tile("inv_sum", [P, 1], F32)
         nc.vector.reciprocal(out=inv_sum[:], in_=row_sum[:])
-        weight = tile("weight", [P, PACK, P], F32)
-        nc.vector.tensor_scalar(out=weight[:], in0=prob[:], scalar1=inv_sum[:], scalar2=None, op0=ALU.mult)
-        weight_t = ps.tile([P, PACK, Q], F32, name="weight_t", tag="soft")
-        for t in range(PACK):
-            nc.tensor.transpose(weight_t[:, t, :], weight[:, t, :], ident[:])
-        wt_bf = tile("wt_bf", [P, Q, PACK], BF16)
-        nc.vector.tensor_tensor(out=wt_bf[:], in0=weight_t[:].rearrange("s t q -> s q t"),
-                                in1=os_t[:].unsqueeze(1).to_broadcast([P, Q, PACK]), op=ALU.mult)
-        wt_codes, wt_scales = quantise("wt", wt_bf[:].rearrange("s q t -> s (q t)"))
+        weight = tile("weight", [P, I], BF16)
+        nc.vector.scalar_tensor_tensor(out=weight[:], in0=prob[:].rearrange("q u s e -> q (u s e)"), scalar=inv_sum[:],
+                                       in1=os_rows[:].rearrange("q u s e -> q (u s e)"), op0=ALU.mult, op1=ALU.mult)
+        weight_pairs = weight[:].bitcast(F32)
+        weight_t = ps.tile([P, 2, Q], F32, name="weight_t", tag="soft")
+        for u in range(2):
+            nc.tensor.transpose(weight_t[:, u, :], weight_pairs[:, u * P : (u + 1) * P], ident[:])
+        wt_bf = tile("wt_bf", [P, Q * PACK], BF16)
+        nc.scalar.copy(out=wt_bf[:].bitcast(F32).rearrange("s (q u) -> s q u", u=2), in_=weight_t[:].rearrange("s u q -> s q u"))
+        wt_codes, wt_scales = quantise("wt", wt_bf[:])
 
-        stage2 = tile("stage2", [P, I + P], F32)
-        stage3 = tile("stage3", [P, I + P], F32)
-        zh3 = layer(3, w_op23)
-        page_sums(zh2, sums2)
-        page_sums(zh3, sums3)
-        hv0 = squash(0, arg0)
-        spread_shift(1, sums1[:], shift1)
-        arg1 = turn(1, shift1, zs1)
-        spread_shift(2, sums2, stage2[:, I:])
-        deal(zh2, stage2[:, :I])
-        spread_shift(3, sums3, stage3[:, I:])
-        deal(zh3, stage3[:, :I])
-        arg2 = turn(2, stage2[:, I:], stage2[:, :I])
-        hv1 = squash(1, arg1)
-        arg3 = turn(3, stage3[:, I:], stage3[:, :I])
-        hv2 = squash(2, arg2)
-        hv3 = squash(3, arg3)
-        for j, hv in enumerate((hv0, hv1, hv2, hv3)):
-            scale_values(j, hv)
-        h_ops = [quantise(f"ht{j}", ht_bf[:, j * I : (j + 1) * I]) for j in range(R_TILES)]
+        sums3 = page_sums(3, zh3)
+        hv0 = squash(0, arg0, AT_KEYS_W + 2048)
+        shift2 = spread_shift(2, sums2)
+        arg2 = turn_and_add(2, shift2, deal(2, zh2))
+        arg3 = shift_and_turn(3, sums3, zh3)
+        hvs = [hv0, squash(1, arg1), squash(2, arg2), squash(3, arg3)]
+        ht_bf = tile("ht_bf", [P, R * PACK], BF16)
         for j in range(R_TILES):
-            read(j, j + 1, h_ops[j])
+            scale_values(hvs[j], ht_bf[:, j * I : (j + 1) * I])
+        h_op01 = quantise("ht01", ht_bf[:, : 2 * I])
+        h_op2 = quantise("ht2", ht_bf[:, 2 * I : 3 * I])
+        h_op3 = quantise("ht3", ht_bf[:, 3 * I :])
+        read(0, h_op01, "acc", 2, nc.scalar.copy)
+        read(2, h_op2, "acc", 2, nc.scalar.copy)
+        read(3, h_op3, "zh", 3, nc.vector.tensor_copy)

@@ -25,6 +25,10 @@ W_HALVES = 2
 KEYS_ROW = 4
 
 
+def column_pieces(pieces):
+    return [slice(n * P // pieces, (n + 1) * P // pieces) for n in range(pieces)]
+
+
 def tile_attend_lrcentred_soft_kernel(tc, query, keys_words, keys_scales, tab_words, tab_scales, w1, share, slot_factor, value_scale, offs, out):
     nc = tc.nc
     with ExitStack() as ctx:
@@ -37,13 +41,13 @@ def tile_attend_lrcentred_soft_kernel(tc, query, keys_words, keys_scales, tab_wo
                 return sb.tile(shape, dtype, name=name, align_bytes=64)
             return reused.tile(shape, dtype, name=name, align_bytes=64, offset=at)
 
-        AT_TAB_S, AT_KEYS_S, AT_Q, AT_W, AT_KEYS_W = 0, 2048, 4096, 4096, 12288
+        AT_TAB_S, AT_KEYS_S, AT_W, AT_KEYS_W, AT_TAB_W = 0, 2048, 4096, 12288, 20480
         G = I // PAGE
 
         offsets = sb.tile([P, I // 16], U16, name="offsets")
         keys_w = tile("keys_w", [P, T], U32, AT_KEYS_W)
         keys_s = tile("keys_s", [P, T], U8, AT_KEYS_S)
-        tab_w = tile("tab_w", [P, T], U32)
+        tab_w = tile("tab_w", [P, T], U32, AT_TAB_W)
         tab_s = tile("tab_s", [P, T], U8, AT_TAB_S)
         q_raw = tile("q_raw", [P, PACK, Q], F32)
         w_raw = [tile("w_raw0", [P, PACK, R // W_HALVES], F32), tile("w_raw1", [P, PACK, R // W_HALVES], F32, AT_W)]
@@ -53,14 +57,15 @@ def tile_attend_lrcentred_soft_kernel(tc, query, keys_words, keys_scales, tab_wo
         ident = tile("ident", [P, P], F32)
 
         nc.vector.memset(tab_s[:].bitcast(I32), 0)
-        nc.vector.memset(keys_s[:].bitcast(I32), 0)
+        nc.gpsimd.memset(keys_s[:].bitcast(I32), 0)
+        nc.gpsimd.memset(share_rows[:], 0.0)
 
         def load_words(dst, words):
             nc.sync.dma_start(out=dst[:].bitcast(I32), in_=words[0].rearrange("p n t -> p (n t)").bitcast(I32))
 
-        def load_scales(dst, scales, first):
+        def load_scales(queue, dst, scales, first):
             for r in range(4):
-                nc.sync.dma_start(out=dst[first + r : P : 32, :].bitcast(I32), in_=scales[0, r:16:4, :].bitcast(I32))
+                queue.dma_start(out=dst[first + r : P : 32, :].bitcast(I32), in_=scales[0, r:16:4, :].bitcast(I32))
 
         def load_w1(h):
             cols = slice(h * (R // W_HALVES), (h + 1) * (R // W_HALVES))
@@ -68,20 +73,19 @@ def tile_attend_lrcentred_soft_kernel(tc, query, keys_words, keys_scales, tab_wo
 
         nc.sync.dma_start(offsets[:], offs)
         load_w1(0)
-        load_scales(tab_s, tab_scales, 0)
+        load_scales(nc.sync, tab_s, tab_scales, 0)
         load_words(tab_w, tab_words)
         nc.sync.dma_start(out=q_raw[:], in_=query.rearrange("(p j) q -> p j q", j=PACK))
-        load_scales(keys_s, keys_scales, KEYS_ROW)
+        nc.sync.dma_start(out=share_rows[0:R_TILES, :], in_=share.rearrange("(j p) o -> j (p o)", p=P))
+        nc.sync.dma_start(out=os_t[:], in_=slot_factor.rearrange("o (p t) -> p (o t)", t=PACK))
         load_w1(1)
         load_words(keys_w, keys_words)
         nc.sync.dma_start(out=vs_t[:], in_=value_scale.rearrange("o (p t) -> p (o t)", t=PACK))
-        nc.gpsimd.memset(share_rows[:], 0.0)
-        nc.gpsimd.dma_start(out=share_rows[0:R_TILES, :], in_=share.rearrange("(j p) o -> j (p o)", p=P))
-        nc.gpsimd.dma_start(out=os_t[:], in_=slot_factor.rearrange("o (p t) -> p (o t)", t=PACK))
+        load_scales(nc.gpsimd, keys_s, keys_scales, KEYS_ROW)
         make_identity(nc, ident[:])
 
-        def gather(name, window, dtype):
-            picked = tile(name, [P, I], dtype)
+        def gather(name, window, dtype, at=None):
+            picked = tile(name, [P, I], dtype, at)
             nc.vector.tensor_copy(picked[:], window[:].indirect(offsets[:]))
             return picked
 
@@ -144,14 +148,16 @@ def tile_attend_lrcentred_soft_kernel(tc, query, keys_words, keys_scales, tab_wo
                 nc.tensor.transpose(arg[:, t, :], centred[:, t].rearrange("r g c -> r (g c)"), ident[:])
             return arg
 
-        def squash(j, arg, at=None):
+        def squash(j, arg, at=None, pieces=1):
             hv = tile(f"hv{j}", [P, P, PACK], F32, at)
-            nc.scalar.activation(out=hv[:], in_=arg[:].rearrange("s t r -> s r t"), func=ACT.Tanh)
+            for cols in column_pieces(pieces):
+                nc.scalar.activation(out=hv[:, cols, :], in_=arg[:, :, cols].rearrange("s t r -> s r t"), func=ACT.Tanh)
             return hv
 
-        def scale_values(hv, ht_bf):
-            nc.vector.tensor_tensor(out=ht_bf.rearrange("s (r t) -> s r t", t=PACK), in0=hv[:],
-                                    in1=vs_t[:].unsqueeze(1).to_broadcast([P, P, PACK]), op=ALU.mult)
+        def scale_values(hv, ht_bf, pieces=1):
+            for cols in column_pieces(pieces):
+                nc.vector.tensor_tensor(out=ht_bf.rearrange("s (r t) -> s r t", t=PACK)[:, cols, :], in0=hv[:, cols, :],
+                                        in1=vs_t[:].unsqueeze(1).to_broadcast([P, P // pieces, PACK]), op=ALU.mult)
 
         def read(j0, h_op, bank, bufs, copy):
             codes, scales = h_op
@@ -175,7 +181,7 @@ def tile_attend_lrcentred_soft_kernel(tc, query, keys_words, keys_scales, tab_wo
         zh1 = layer(1, w01_codes[:, P:], w01_scales[:, P:])
         q_bf = tile("q_bf", [P, Q * PACK], BF16)
         interleave(q_bf[:], q_raw[:])
-        keys_sg = gather("keys_sg", keys_s, U8)
+        keys_sg = gather("keys_sg", keys_s, U8, AT_TAB_W)
         w_bf23 = w1_bf(1)
         pull = tile("pull", [P, R_TILES], F32, AT_W + 3200)
         nc.scalar.activation(out=pull[:], in_=share_cols[:, :R_TILES], func=ACT.Copy, scale=-1.0 / PAGE)
@@ -223,10 +229,10 @@ def tile_attend_lrcentred_soft_kernel(tc, query, keys_words, keys_scales, tab_wo
         shift2 = spread_shift(2, sums2)
         arg2 = turn_and_add(2, shift2, deal(2, zh2))
         arg3 = shift_and_turn(3, sums3, zh3)
-        hvs = [hv0, squash(1, arg1), squash(2, arg2), squash(3, arg3)]
+        hvs = [hv0, squash(1, arg1), squash(2, arg2), squash(3, arg3, pieces=2)]
         ht_bf = tile("ht_bf", [P, R * PACK], BF16)
         for j in range(R_TILES):
-            scale_values(hvs[j], ht_bf[:, j * I : (j + 1) * I])
+            scale_values(hvs[j], ht_bf[:, j * I : (j + 1) * I], 2 if j == R_TILES - 1 else 1)
         h_op01 = quantise("ht01", ht_bf[:, : 2 * I])
         h_op2 = quantise("ht2", ht_bf[:, 2 * I : 3 * I])
         h_op3 = quantise("ht3", ht_bf[:, 3 * I :])

@@ -41,31 +41,31 @@ def tile_attend_lrcentred_soft_kernel(tc, query, keys_words, keys_scales, tab_wo
                 return sb.tile(shape, dtype, name=name, align_bytes=64)
             return reused.tile(shape, dtype, name=name, align_bytes=64, offset=at)
 
-        AT_TAB_S, AT_KEYS_S, AT_W, AT_KEYS_W, AT_TAB_W = 0, 2048, 4096, 12288, 20480
+        AT_TAB_S, AT_KEYS_S, AT_W, AT_KEYS_W = 0, 2048, 4096, 8192
         G = I // PAGE
 
         offsets = sb.tile([P, I // 16], U16, name="offsets")
         keys_w = tile("keys_w", [P, T], U32, AT_KEYS_W)
         keys_s = tile("keys_s", [P, T], U8, AT_KEYS_S)
-        tab_w = tile("tab_w", [P, T], U32, AT_TAB_W)
+        tab_w = tile("tab_w", [P, T], U32)
         tab_s = tile("tab_s", [P, T], U8, AT_TAB_S)
         q_raw = tile("q_raw", [P, PACK, Q], F32)
         w_raw = [tile("w_raw0", [P, PACK, R // W_HALVES], F32), tile("w_raw1", [P, PACK, R // W_HALVES], F32, AT_W)]
         share_rows = tile("share_rows", [P, P], F32)
-        os_t = tile("os_t", [P, PACK], F32)
+        os_rows = tile("os_rows", [P, I], F32)
         vs_t = tile("vs_t", [P, PACK], F32)
         ident = tile("ident", [P, P], F32)
 
         nc.vector.memset(tab_s[:].bitcast(I32), 0)
-        nc.gpsimd.memset(keys_s[:].bitcast(I32), 0)
+        nc.vector.memset(keys_s[:].bitcast(I32), 0)
         nc.gpsimd.memset(share_rows[:], 0.0)
 
         def load_words(dst, words):
             nc.sync.dma_start(out=dst[:].bitcast(I32), in_=words[0].rearrange("p n t -> p (n t)").bitcast(I32))
 
-        def load_scales(queue, dst, scales, first):
+        def load_scales(dst, scales, first):
             for r in range(4):
-                queue.dma_start(out=dst[first + r : P : 32, :].bitcast(I32), in_=scales[0, r:16:4, :].bitcast(I32))
+                nc.sync.dma_start(out=dst[first + r : P : 32, :].bitcast(I32), in_=scales[0, r:16:4, :].bitcast(I32))
 
         def load_w1(h):
             cols = slice(h * (R // W_HALVES), (h + 1) * (R // W_HALVES))
@@ -73,19 +73,19 @@ def tile_attend_lrcentred_soft_kernel(tc, query, keys_words, keys_scales, tab_wo
 
         nc.sync.dma_start(offsets[:], offs)
         load_w1(0)
-        load_scales(nc.sync, tab_s, tab_scales, 0)
+        load_scales(tab_s, tab_scales, 0)
         load_words(tab_w, tab_words)
         nc.sync.dma_start(out=q_raw[:], in_=query.rearrange("(p j) q -> p j q", j=PACK))
         nc.sync.dma_start(out=share_rows[0:R_TILES, :], in_=share.rearrange("(j p) o -> j (p o)", p=P))
-        nc.sync.dma_start(out=os_t[:], in_=slot_factor.rearrange("o (p t) -> p (o t)", t=PACK))
+        load_scales(keys_s, keys_scales, KEYS_ROW)
         load_w1(1)
         load_words(keys_w, keys_words)
         nc.sync.dma_start(out=vs_t[:], in_=value_scale.rearrange("o (p t) -> p (o t)", t=PACK))
-        load_scales(nc.gpsimd, keys_s, keys_scales, KEYS_ROW)
+        nc.sync.dma_start(out=os_rows[:], in_=slot_factor[0].partition_broadcast(P))
         make_identity(nc, ident[:])
 
-        def gather(name, window, dtype, at=None):
-            picked = tile(name, [P, I], dtype, at)
+        def gather(name, window, dtype):
+            picked = tile(name, [P, I], dtype)
             nc.vector.tensor_copy(picked[:], window[:].indirect(offsets[:]))
             return picked
 
@@ -169,9 +169,6 @@ def tile_attend_lrcentred_soft_kernel(tc, query, keys_words, keys_scales, tab_wo
             copy(out=res[:], in_=acc[:])
             nc.sync.dma_start(out=out[:, j0 * P : j0 * P + width], in_=res[:])
 
-        os_spread = ps.tile([P, PACK, P], F32, name="os_spread", tag="acc", bufs=2)
-        for t in range(PACK):
-            nc.tensor.transpose(os_spread[:, t, :], os_t[:, t : t + 1].to_broadcast([P, P]), ident[:])
         share_cols = ps.tile([P, P], F32, name="share_cols", tag="acc", bufs=2)
         nc.tensor.transpose(share_cols[:], share_rows[:], ident[:])
         tab_sg = gather("tab_sg", tab_s, U8)
@@ -181,7 +178,7 @@ def tile_attend_lrcentred_soft_kernel(tc, query, keys_words, keys_scales, tab_wo
         zh1 = layer(1, w01_codes[:, P:], w01_scales[:, P:])
         q_bf = tile("q_bf", [P, Q * PACK], BF16)
         interleave(q_bf[:], q_raw[:])
-        keys_sg = gather("keys_sg", keys_s, U8, AT_TAB_W)
+        keys_sg = gather("keys_sg", keys_s, U8)
         w_bf23 = w1_bf(1)
         pull = tile("pull", [P, R_TILES], F32, AT_W + 3200)
         nc.scalar.activation(out=pull[:], in_=share_cols[:, :R_TILES], func=ACT.Copy, scale=-1.0 / PAGE)
@@ -193,8 +190,6 @@ def tile_attend_lrcentred_soft_kernel(tc, query, keys_words, keys_scales, tab_wo
         arg0 = turn_and_add(0, zs0, spread_shift(0, sums0, AT_W + 2048))
         sums1 = page_sums(1, zh1, AT_W + 2560)
         zs1 = deal(1, zh1)
-        os_rows = tile("os_rows", [P, 2, P, 2], F32, AT_W + 3264)
-        nc.scalar.copy(out=os_rows[:], in_=os_spread[:].rearrange("q (u e) s -> q u s e", e=2))
 
         keys_g = gather("keys_g", keys_w, U32)
         scores = ps.tile([P, I], F32, name="scores", tag="soft")
@@ -213,13 +208,13 @@ def tile_attend_lrcentred_soft_kernel(tc, query, keys_words, keys_scales, tab_wo
                              bias=neg_max[:], accum_out=row_sum[:])
         inv_sum = tile("inv_sum", [P, 1], F32)
         nc.vector.reciprocal(out=inv_sum[:], in_=row_sum[:])
-        weight = tile("weight", [P, I], BF16)
-        nc.vector.scalar_tensor_tensor(out=weight[:], in0=prob[:].rearrange("q u s e -> q (u s e)"), scalar=inv_sum[:],
-                                       in1=os_rows[:].rearrange("q u s e -> q (u s e)"), op0=ALU.mult, op1=ALU.mult)
-        weight_pairs = weight[:].bitcast(F32)
+        weight = tile("weight", [P, 2, P, 2], BF16)
+        os_pairs = os_rows[:].rearrange("q (s u e) -> q u s e", u=2, e=2)
         weight_t = ps.tile([P, 2, Q], F32, name="weight_t", tag="soft")
         for u in range(2):
-            nc.tensor.transpose(weight_t[:, u, :], weight_pairs[:, u * P : (u + 1) * P], ident[:])
+            nc.vector.scalar_tensor_tensor(out=weight[:, u], in0=prob[:, u], scalar=inv_sum[:], in1=os_pairs[:, u],
+                                           op0=ALU.mult, op1=ALU.mult)
+            nc.tensor.transpose(weight_t[:, u, :], weight[:, u].rearrange("q s e -> q (s e)").bitcast(F32), ident[:])
         wt_bf = tile("wt_bf", [P, Q * PACK], BF16)
         nc.scalar.copy(out=wt_bf[:].bitcast(F32).rearrange("s (q u) -> s q u", u=2), in_=weight_t[:].rearrange("s u q -> s q u"))
         wt_codes, wt_scales = quantise("wt", wt_bf[:])

@@ -176,17 +176,20 @@ def tile_attend_lrcentred_soft_kernel(tc, query, keys_words, keys_scales, tab_wo
         tab_g = gather("tab_g", tab_w, U32)
         zh0 = layer(0, w01_codes[:, :P], w01_scales[:, :P])
         zh1 = layer(1, w01_codes[:, P:], w01_scales[:, P:])
+        warm = ps.tile([P, I], F32, name="warm", tag="soft")
+        nc.tensor.matmul_mx(out=warm[:], lhsT=w01_codes[:, P:].bitcast(FP8X4), lhsT_scale=w01_scales[:, P:],
+                            rhs=tab_g[:].bitcast(FP8X4), rhs_scale=tab_sg[:], start=True, stop=True)
         q_bf = tile("q_bf", [P, Q * PACK], BF16)
         interleave(q_bf[:], q_raw[:])
         keys_sg = gather("keys_sg", keys_s, U8)
         w_bf23 = w1_bf(1)
-        pull = tile("pull", [P, R_TILES], F32, AT_W + 3200)
-        nc.scalar.activation(out=pull[:], in_=share_cols[:, :R_TILES], func=ACT.Copy, scale=-1.0 / PAGE)
         sums0 = page_sums(0, zh0, AT_KEYS_S)
         w2_codes, w2_scales = quantise("w2", w_bf23[:, : P * PACK])
         zh2 = layer(2, w2_codes[:], w2_scales[:])
         q_codes, q_scales = quantise("q", q_bf[:], AT_W + 2688)
         zs0 = deal(0, zh0, AT_W)
+        pull = tile("pull", [P, R_TILES], F32, AT_W + 3200)
+        nc.scalar.activation(out=pull[:], in_=share_cols[:, :R_TILES], func=ACT.Copy, scale=-1.0 / PAGE)
         arg0 = turn_and_add(0, zs0, spread_shift(0, sums0, AT_W + 2048))
         sums1 = page_sums(1, zh1, AT_W + 2560)
         zs1 = deal(1, zh1)

from contextlib import ExitStack

import concourse.mybir as mybir
from concourse.masks import make_identity

D, K, R, T, I, Q = 512, 512, 512, 2048, 512, 128
PAGE = 16
FLOPS = 2 * (Q * D * I + R * K * I + Q * I * R)

F32 = mybir.dt.float32
BF16 = mybir.dt.bfloat16
I32 = mybir.dt.int32
U32 = mybir.dt.uint32
U16 = mybir.dt.uint16
U8 = mybir.dt.uint8
FP8X4 = mybir.dt.float8_e4m3fn_x4
ACT = mybir.ActivationFunctionType
ALU = mybir.AluOpType
AX = mybir.AxisListType

P = 128
PACK = 4
R_TILES = R // P
W_HALVES = 2
KEYS_ROW = 4


def column_pieces(pieces):
    return [slice(n * P // pieces, (n + 1) * P // pieces) for n in range(pieces)]


def tile_attend_lrcentred_soft_kernel(tc, query, keys_words, keys_scales, tab_words, tab_scales, w1, share, slot_factor, value_scale, offs, out):
    nc = tc.nc
    with ExitStack() as ctx:
        sb = ctx.enter_context(tc.tile_pool(name="sb", bufs=1))
        reused = ctx.enter_context(tc.tile_pool(name="reused", bufs=1))
        ps = ctx.enter_context(tc.psum_pool(name="ps", bufs=1))

        def tile(name, shape, dtype, at=None):
            if at is None:
                return sb.tile(shape, dtype, name=name, align_bytes=64)
            return reused.tile(shape, dtype, name=name, align_bytes=64, offset=at)

        AT_TAB_S, AT_KEYS_S, AT_W, AT_KEYS_W = 0, 2048, 4096, 8192
        G = I // PAGE

        offsets = sb.tile([P, I // 16], U16, name="offsets")
        keys_w = tile("keys_w", [P, T], U32, AT_KEYS_W)
        keys_s = tile("keys_s", [P, T], U8, AT_KEYS_S)
        tab_w = tile("tab_w", [P, T], U32)
        tab_s = tile("tab_s", [P, T], U8, AT_TAB_S)
        q_raw = tile("q_raw", [P, PACK, Q], F32)
        w_raw = [tile("w_raw0", [P, PACK, R // W_HALVES], F32), tile("w_raw1", [P, PACK, R // W_HALVES], F32, AT_W)]
        share_rows = tile("share_rows", [P, P], F32)
        os_rows = tile("os_rows", [P, I], F32)
        vs_t = tile("vs_t", [P, PACK], F32)
        ident = tile("ident", [P, P], F32)

        nc.vector.memset(tab_s[:].bitcast(I32), 0)
        nc.vector.memset(keys_s[:].bitcast(I32), 0)
        nc.gpsimd.memset(share_rows[:], 0.0)

        def load_words(dst, words):
            nc.sync.dma_start(out=dst[:].bitcast(I32), in_=words[0].rearrange("p n t -> p (n t)").bitcast(I32))

        def load_scales(dst, scales, first):
            for r in range(4):
                nc.sync.dma_start(out=dst[first + r : P : 32, :].bitcast(I32), in_=scales[0, r:16:4, :].bitcast(I32))

        def load_w1(h):
            cols = slice(h * (R // W_HALVES), (h + 1) * (R // W_HALVES))
            nc.sync.dma_start(out=w_raw[h][:], in_=w1[:, cols].rearrange("(p j) c -> p j c", j=PACK))

        nc.sync.dma_start(offsets[:], offs)
        load_w1(0)
        load_scales(tab_s, tab_scales, 0)
        load_words(tab_w, tab_words)
        nc.sync.dma_start(out=q_raw[:], in_=query.rearrange("(p j) q -> p j q", j=PACK))
        nc.sync.dma_start(out=share_rows[0:R_TILES, :], in_=share.rearrange("(j p) o -> j (p o)", p=P))
        load_scales(keys_s, keys_scales, KEYS_ROW)
        load_w1(1)
        load_words(keys_w, keys_words)
        nc.sync.dma_start(out=vs_t[:], in_=value_scale.rearrange("o (p t) -> p (o t)", t=PACK))
        nc.sync.dma_start(out=os_rows[:], in_=slot_factor[0].partition_broadcast(P))
        make_identity(nc, ident[:])

        def gather(name, window, dtype):
            picked = tile(name, [P, I], dtype)
            nc.vector.tensor_copy(picked[:], window[:].indirect(offsets[:]))
            return picked

        def interleave(grouped, raw):
            nc.scalar.activation(
                out=grouped.rearrange("p (c i t) -> p c t i", i=4, t=PACK),
                in_=raw.rearrange("p t (c i) -> p c t i", i=4),
                func=ACT.Copy,
            )

        def quantise(name, grouped, at=None):
            width = grouped.shape[1] // PACK
            codes = tile(name + "_codes", [P, width], U32, at)
            scales = tile(name + "_scales", [P, width], U8)
            nc.vector.quantize_mx(out=codes[:].bitcast(FP8X4), scales=scales[:], in_=grouped)
            return codes, scales

        def w1_bf(h):
            grouped = tile(f"w_bf{h}", [P, 2 * P * PACK], BF16)
            for e in range(2):
                interleave(grouped[:, e * P * PACK : (e + 1) * P * PACK], w_raw[h][:, :, e * P : (e + 1) * P])
            return grouped

        def layer(j, codes, scales):
            zh = ps.tile([P, I], F32, name=f"zh{j}", tag="zh", bufs=3)
            nc.tensor.matmul_mx(out=zh[:], lhsT=codes.bitcast(FP8X4), lhsT_scale=scales,
                                rhs=tab_g[:].bitcast(FP8X4), rhs_scale=tab_sg[:], start=True, stop=True)
            return zh

        def page_sums(j, zh, at=None):
            sums = tile(f"sums{j}", [P, G], F32, at)
            nc.vector.tensor_reduce(out=sums[:], in_=zh[:].rearrange("r (g u) -> r g u", u=PAGE), axis=AX.X, op=ALU.add)
            return sums[:].unsqueeze(2).to_broadcast([P, G, PAGE // PACK])

        def spread_shift(j, sums, at=None):
            shift = tile(f"shift{j}", [P, G, PAGE // PACK], F32, at)
            nc.scalar.activation(out=shift[:], in_=sums, func=ACT.Copy, scale=pull[:, j : j + 1])
            return [shift[:].rearrange("r g c -> r (g c)")] * PACK

        def deal(j, zh, at=None):
            zs = tile(f"zs{j}", [P, PACK, P], F32, at)
            nc.scalar.copy(out=zs[:], in_=zh[:].rearrange("r (s t) -> r t s", t=PACK))
            return [zs[:, t, :] for t in range(PACK)]

        def turn_and_add(j, first, second):
            arg = ps.tile([P, PACK, P], F32, name=f"arg{j}", tag="arg", bufs=2)
            for t in range(PACK):
                nc.tensor.matmul(arg[:, t, :], lhsT=first[t], rhs=ident[:], is_transpose=True, start=(t == 0), stop=False)
            for t in range(PACK):
                nc.tensor.matmul(arg[:, t, :], lhsT=second[t], rhs=ident[:], is_transpose=True, start=False, stop=(t == PACK - 1))
            return arg

        def shift_and_turn(j, sums, zh):
            centred = tile(f"centred{j}", [P, PACK, G, PAGE // PACK], F32)
            by_place = zh[:].rearrange("r (g c t) -> r t g c", c=PAGE // PACK, t=PACK)
            arg = ps.tile([P, PACK, P], F32, name=f"arg{j}", tag="arg", bufs=2)
            for t in range(PACK):
                nc.vector.scalar_tensor_tensor(out=centred[:, t], in0=sums, scalar=pull[:, j : j + 1], in1=by_place[:, t],
                                               op0=ALU.mult, op1=ALU.add)
                nc.tensor.transpose(arg[:, t, :], centred[:, t].rearrange("r g c -> r (g c)"), ident[:])
            return arg

        def squash(j, arg, at=None, pieces=1):
            hv = tile(f"hv{j}", [P, P, PACK], F32, at)
            for cols in column_pieces(pieces):
                nc.scalar.activation(out=hv[:, cols, :], in_=arg[:, :, cols].rearrange("s t r -> s r t"), func=ACT.Tanh)
            return hv

        def scale_values(hv, ht_bf, pieces=1):
            for cols in column_pieces(pieces):
                nc.vector.tensor_tensor(out=ht_bf.rearrange("s (r t) -> s r t", t=PACK)[:, cols, :], in0=hv[:, cols, :],
                                        in1=vs_t[:].unsqueeze(1).to_broadcast([P, P // pieces, PACK]), op=ALU.mult)

        def read(j0, h_op, bank, bufs, copy):
            codes, scales = h_op
            width = codes.shape[1]
            acc = ps.tile([P, width], F32, name=f"acc{j0}", tag=bank, bufs=bufs)
            nc.tensor.matmul_mx(out=acc[:], lhsT=wt_codes[:].bitcast(FP8X4), lhsT_scale=wt_scales[:],
                                rhs=codes[:].bitcast(FP8X4), rhs_scale=scales[:], start=True, stop=True)
            res = tile(f"res{j0}", [P, width], F32)
            copy(out=res[:], in_=acc[:])
            nc.sync.dma_start(out=out[:, j0 * P : j0 * P + width], in_=res[:])

        share_cols = ps.tile([P, P], F32, name="share_cols", tag="acc", bufs=2)
        nc.tensor.transpose(share_cols[:], share_rows[:], ident[:])
        tab_sg = gather("tab_sg", tab_s, U8)
        w01_codes, w01_scales = quantise("w01", w1_bf(0)[:], AT_TAB_S)
        tab_g = gather("tab_g", tab_w, U32)
        zh0 = layer(0, w01_codes[:, :P], w01_scales[:, :P])
        zh1 = layer(1, w01_codes[:, P:], w01_scales[:, P:])
        warm = ps.tile([P, I], F32, name="warm", tag="soft")
        nc.tensor.matmul_mx(out=warm[:], lhsT=w01_codes[:, P:].bitcast(FP8X4), lhsT_scale=w01_scales[:, P:],
                            rhs=tab_g[:].bitcast(FP8X4), rhs_scale=tab_sg[:], start=True, stop=True)
        q_bf = tile("q_bf", [P, Q * PACK], BF16)
        interleave(q_bf[:], q_raw[:])
        keys_sg = gather("keys_sg", keys_s, U8)
        w_bf23 = w1_bf(1)
        sums0 = page_sums(0, zh0, AT_KEYS_S)
        w2_codes, w2_scales = quantise("w2", w_bf23[:, : P * PACK])
        zh2 = layer(2, w2_codes[:], w2_scales[:])
        q_codes, q_scales = quantise("q", q_bf[:], AT_W + 2688)
        zs0 = deal(0, zh0, AT_W)
        pull = tile("pull", [P, R_TILES], F32, AT_W + 3200)
        nc.scalar.activation(out=pull[:], in_=share_cols[:, :R_TILES], func=ACT.Copy, scale=-1.0 / PAGE)
        arg0 = turn_and_add(0, zs0, spread_shift(0, sums0, AT_W + 2048))
        sums1 = page_sums(1, zh1, AT_W + 2560)
        zs1 = deal(1, zh1)

        keys_g = gather("keys_g", keys_w, U32)
        scores = ps.tile([P, I], F32, name="scores", tag="soft")
        nc.tensor.matmul_mx(out=scores[:], lhsT=q_codes[:].bitcast(FP8X4), lhsT_scale=q_scales[:],
                            rhs=keys_g[:].bitcast(FP8X4), rhs_scale=keys_sg[KEYS_ROW:P, :], start=True, stop=True)
        w3_codes, w3_scales = quantise("w3", w_bf23[:, P * PACK :], AT_KEYS_W)
        zh3 = layer(3, w3_codes[:], w3_scales[:])
        arg1 = turn_and_add(1, spread_shift(1, sums1, AT_KEYS_W + 512), zs1)
        sums2 = page_sums(2, zh2, AT_KEYS_W + 1024)

        neg_max = tile("neg_max", [P, 1], F32)
        nc.vector.tensor_reduce(out=neg_max[:], in_=scores[:], axis=AX.X, op=ALU.max, negate=True)
        prob = tile("prob", [P, 2, P, 2], F32)
        row_sum = tile("row_sum", [P, 1], F32)
        nc.scalar.activation(out=prob[:], in_=scores[:].rearrange("q (s u e) -> q u s e", u=2, e=2), func=ACT.Exp,
                             bias=neg_max[:], accum_out=row_sum[:])
        inv_sum = tile("inv_sum", [P, 1], F32)
        nc.vector.reciprocal(out=inv_sum[:], in_=row_sum[:])
        weight = tile("weight", [P, 2, P, 2], BF16)
        os_pairs = os_rows[:].rearrange("q (s u e) -> q u s e", u=2, e=2)
        weight_t = ps.tile([P, 2, Q], F32, name="weight_t", tag="soft")
        for u in range(2):
            nc.vector.scalar_tensor_tensor(out=weight[:, u], in0=prob[:, u], scalar=inv_sum[:], in1=os_pairs[:, u],
                                           op0=ALU.mult, op1=ALU.mult)
            nc.tensor.transpose(weight_t[:, u, :], weight[:, u].rearrange("q s e -> q (s e)").bitcast(F32), ident[:])
        wt_bf = tile("wt_bf", [P, Q * PACK], BF16)
        nc.scalar.copy(out=wt_bf[:].bitcast(F32).rearrange("s (q u) -> s q u", u=2), in_=weight_t[:].rearrange("s u q -> s q u"))
        wt_codes, wt_scales = quantise("wt", wt_bf[:])

        sums3 = page_sums(3, zh3)
        hv0 = squash(0, arg0, AT_KEYS_W + 2048)
        shift2 = spread_shift(2, sums2)
        arg2 = turn_and_add(2, shift2, deal(2, zh2))
        arg3 = shift_and_turn(3, sums3, zh3)
        hvs = [hv0, squash(1, arg1), squash(2, arg2), squash(3, arg3, pieces=2)]
        ht_bf = tile("ht_bf", [P, R * PACK], BF16)
        for j in range(R_TILES):
            scale_values(hvs[j], ht_bf[:, j * I : (j + 1) * I], 2 if j == R_TILES - 1 else 1)
        h_op01 = quantise("ht01", ht_bf[:, : 2 * I])
        h_op2 = quantise("ht2", ht_bf[:, 2 * I : 3 * I])
        h_op3 = quantise("ht3", ht_bf[:, 3 * I :])
        read(0, h_op01, "acc", 2, nc.scalar.copy)
        read(2, h_op2, "acc", 2, nc.scalar.copy)
        read(3, h_op3, "zh", 3, nc.vector.tensor_copy)
